import numpy as np
import ml_dtypes


def mxq(x, axis, fmt="e4m3"):
    dtype, down = {"e4m3": (ml_dtypes.float8_e4m3fn, 7), "e5m2": (ml_dtypes.float8_e5m2, 14)}[fmt]
    v = np.moveaxis(np.asarray(x, np.float32).astype(ml_dtypes.bfloat16).astype(np.float64), axis, -1)
    blocks = v.reshape(v.shape[:-1] + (-1, 32))
    amax = np.abs(blocks).max(-1, keepdims=True)
    byte = np.maximum(np.where(amax > 0, np.frexp(amax)[1] - 1 + 127, 0) - down, 1)
    scale = np.exp2(byte - 127.0)
    codes = (blocks / scale).astype(np.float32).astype(dtype).astype(np.float64)
    return np.moveaxis((codes * scale).reshape(v.shape), -1, axis)


WIDE = False


def mx_kscale(k):
    if not WIDE:
        return np.ones(k)
    levels = np.array([10, -10, 5, -5, 0])
    if k % 512:
        return np.exp2(np.random.permutation(np.resize(levels, k // 32))).repeat(32)
    a = np.empty((k // 512, 16))
    for p in range(k // 512):
        a[p, :8] = np.random.permutation(np.resize(levels, 8))
        for g in range(8):
            far = levels[np.abs(levels - a[p, g]) >= 10]
            a[p, g + 8] = far[np.random.randint(len(far))]
    return np.exp2(a.ravel()).repeat(32)


def f64(x):
    return np.asarray(x).astype(np.float64)


def striped(idx):
    return np.tile(idx.reshape(-1, 16).T, (8, 1)).astype(np.uint16)


def unstriped(offs):
    return offs[:16].T.reshape(-1).astype(np.int64)


def pack_weight(w):
    k, n = w.shape
    w = f64(np.asarray(w, np.float32).astype(ml_dtypes.bfloat16)).reshape(k // 32, 32, n)
    amax = np.abs(w).max(1)
    byte = np.clip(np.where(amax > 0, np.frexp(amax)[1] - 1 + 127 - 7, 1), 1, 254)
    scaled = (w * np.exp2(127.0 - byte)[:, None, :]).reshape(k, n).astype(np.float32)
    words = np.ascontiguousarray(scaled.reshape(k // 512, 128, 4, n).transpose(0, 1, 3, 2)).astype(ml_dtypes.float8_e4m3fn).view(np.uint8)
    return words, np.ascontiguousarray(byte.astype(np.uint8).reshape(k // 512, 16, n))


def unpack_weight(words, scales):
    g, p, n, _ = words.shape
    vals = np.ascontiguousarray(words).view(ml_dtypes.float8_e4m3fn).astype(np.float64) * np.repeat(np.exp2(scales.astype(np.float64) - 127.0), 8, axis=1)[..., None]
    return vals.transpose(0, 1, 3, 2).reshape(g * 512, n)


def planes(y):
    n, m = y.shape
    v = y.astype(np.float32).astype(ml_dtypes.bfloat16).astype(np.float64).reshape(n // 32, 32, m)
    top = np.abs(v).max(1)
    byte = np.clip(np.where(top > 0, np.frexp(top)[1] - 1 + 127 - 7, 1), 1, 254)
    codes = (v * np.exp2(127.0 - byte)[:, None, :]).reshape(n, m).astype(np.float32).astype(ml_dtypes.float8_e4m3fn).view(np.uint8)
    words = codes.reshape(n // 512, 128, 4, m).transpose(0, 1, 3, 2)
    return np.ascontiguousarray(words), np.ascontiguousarray(byte.astype(np.uint8).reshape(n // 512, 16, m))


K, T, S, J = 1024, 4096, 1024, 512


def setup_inputs():
    n = np.random.standard_normal
    s = mx_kscale(K)[:, None]
    packed_xT = pack_weight(n((K, T)) * s)
    return {
        "x_words": packed_xT[0],
        "x_scales": packed_xT[1],
        "hT": (n((K, J)) / np.sqrt(K) / s).astype(np.float32),
        "label": (np.random.uniform(0.0, 1.0, (S, J))).astype(np.float32),
        "offs": striped(np.random.permutation(T)[:S]),
    }


def reference(x_words, x_scales, hT, label, offs):
    xq = unpack_weight(x_words, x_scales)[:, unstriped(offs)]
    hTq = mxq(f64(hT), 0, "e4m3")
    y = xq.T @ hTq
    out_0 = y - f64(label)
    return (out_0,) + planes(out_0)

@@ -1,0 +1,166 @@
+from contextlib import ExitStack
+
+import concourse.mybir as mybir
+
+K, T, S, J = 1024, 4096, 1024, 512
+FLOPS = 2 * K * S * J
+
+F32 = mybir.dt.float32
+BF16 = mybir.dt.bfloat16
+I32 = mybir.dt.int32
+U32 = mybir.dt.uint32
+U16 = mybir.dt.uint16
+U8 = mybir.dt.uint8
+FP8X4 = mybir.dt.float8_e4m3fn_x4
+
+P = 128
+PACK = 4
+SPAN = P * PACK
+PASSES = K // SPAN
+GROUPS = S // SPAN
+QUADS = 4
+H_SCALAR_COLS = (192, 192)
+Y_SCALAR_COLS = (512, 192)
+
+
+def interleave(copy, grouped, rows, lo, hi):
+    copy(
+        out=grouped[:, PACK * lo : PACK * hi].rearrange("p (c i t) -> p c t i", i=4, t=PACK),
+        in_=rows[:, :, lo:hi].rearrange("p t (c i) -> p c t i", i=4),
+    )
+
+
+def shared_interleave(nc, grouped, rows, scalar_cols):
+    interleave(nc.scalar.copy, grouped, rows, J - scalar_cols, J)
+    if scalar_cols < J:
+        interleave(nc.vector.tensor_copy, grouped, rows, 0, J - scalar_cols)
+
+
+def tile_picked_znceg_sq_po_kernel(tc, x_words, x_scales, hT, label, offs, out_0, out_1, out_2):
+    nc = tc.nc
+    with ExitStack() as ctx:
+        keep = ctx.enter_context(tc.tile_pool(name="keep", bufs=1))
+        psum = ctx.enter_context(tc.psum_pool(name="psum", bufs=1))
+
+        offsets = keep.tile([P, S // 16], U16, name="offsets")
+        nc.sync.dma_start(offsets[:], offs)
+
+        scale_table = keep.tile([P, T], U8, name="scale_table", align_bytes=64)
+        nc.vector.memset(scale_table[:].bitcast(I32), 0)
+
+        word_table = [keep.tile([P, T], U32, name="word_table%d" % o, align_bytes=64) for o in range(PASSES)]
+
+        def load_words(o, lo, hi):
+            nc.sync.dma_start(
+                out=word_table[o][:, lo:hi].bitcast(I32),
+                in_=x_words[o].rearrange("p c t -> p (c t)")[:, PACK * lo : PACK * hi].bitcast(I32),
+            )
+
+        def load_scales(o):
+            for r in range(4):
+                nc.sync.dma_start(
+                    out=scale_table[4 * o + r : P : 32, :].bitcast(I32),
+                    in_=x_scales[o, r:16:4, :].bitcast(I32),
+                )
+
+        load_words(0, 0, T // 4)
+        load_scales(0)
+        load_words(0, T // 4, T // 2)
+        load_scales(1)
+        load_words(0, T // 2, T)
+        load_words(1, 0, T)
+        h_rows = []
+        for o in range(PASSES):
+            rows = keep.tile([P, PACK, J], F32, name="h_rows%d" % o, align_bytes=64)
+            nc.sync.dma_start(
+                out=rows[:], in_=hT[o * SPAN : (o + 1) * SPAN, :].rearrange("(p t) j -> p t j", t=PACK)
+            )
+            h_rows.append(rows)
+        label_rows = []
+        for g in range(GROUPS):
+            dealt = label[g * SPAN : (g + 1) * SPAN, :].rearrange("(p t) j -> p t j", t=PACK)
+            for u in range(2):
+                rows = keep.tile([P, 2, J], F32, name="label_rows%d_%d" % (g, u), align_bytes=64)
+                nc.sync.dma_start(out=rows[:], in_=dealt[:, 2 * u : 2 * u + 2, :])
+                label_rows.append(rows)
+
+        picked_scales = keep.tile([P, S], U8, name="picked_scales", align_bytes=64)
+        nc.vector.tensor_copy(picked_scales[:], scale_table[:].indirect(offsets[:]))
+        picked_words = []
+        x_codes = []
+        for o in range(PASSES):
+            picked_words.append(keep.tile([P, S], U32, name="picked_words%d" % o, align_bytes=64))
+        x_planes = keep.tile([P, S], U8, name="x_planes", align_bytes=64)
+        nc.vector.tensor_copy(
+            out=x_planes[:].rearrange("p (g t c i) -> p g c t i", g=GROUPS, t=PACK, i=16),
+            in_=picked_scales[:].rearrange("p (g c i t) -> p g c t i", g=GROUPS, t=PACK, i=16),
+        )
+
+        def deal_words(o, tag):
+            x_codes.append(keep.tile([P, S], U32, name="x_codes%d" % o, tag=tag, align_bytes=64))
+            nc.vector.tensor_copy(
+                out=x_codes[o][:].bitcast(I32).rearrange("p (g t c i) -> p g c t i", g=GROUPS, t=PACK, i=4),
+                in_=picked_words[o][:].bitcast(I32).rearrange("p (g c i t) -> p g c t i", g=GROUPS, t=PACK, i=4),
+            )
+
+        for o in range(PASSES):
+            nc.vector.tensor_copy(picked_words[o][:], word_table[o][:].indirect(offsets[:]))
+            if o == 0:
+                deal_words(0, "x_codes0")
+
+        h_codes = []
+        h_planes = []
+        h_grouped = keep.tile([P, PACK * (J + H_SCALAR_COLS[1])], BF16, name="h_grouped", align_bytes=64)
+        for o in range(PASSES):
+            first = o * PACK * H_SCALAR_COLS[1]
+            grouped = h_grouped[:, first : first + PACK * J]
+            shared_interleave(nc, grouped, h_rows[o], H_SCALAR_COLS[o])
+            codes = keep.tile([P, J], U32, name="h_codes%d" % o, align_bytes=64)
+            plane = keep.tile([P, J], U8, name="h_plane%d" % o, align_bytes=64)
+            nc.vector.quantize_mx(out=codes[:].bitcast(FP8X4), scales=plane[:], in_=grouped)
+            h_codes.append(codes)
+            h_planes.append(plane)
+            if o == 0:
+                deal_words(1, "h_rows0")
+
+        y_planes = keep.tile([P, GROUPS, J], U8, name="y_planes", align_bytes=64)
+        y_rows = []
+        y_grouped = []
+        for g in range(GROUPS):
+            banks = [psum.tile([P, J], F32, name="bank%d" % t) for t in range(PACK)]
+            order = [(o, t) for o in range(PASSES) for t in range(PACK)]
+            if g > 0:
+                order = sorted(order, key=lambda pair: pair[1])
+            for o, t in order:
+                if True:
+                    cols = slice(g * SPAN + t * P, g * SPAN + (t + 1) * P)
+                    nc.tensor.matmul_mx(
+                        out=banks[t][:],
+                        lhsT=x_codes[o][:, cols].bitcast(FP8X4),
+                        lhsT_scale=x_planes[4 * o : P, cols],
+                        rhs=h_codes[o][:].bitcast(FP8X4),
+                        rhs_scale=h_planes[o][:],
+                        start=(o == 0),
+                        stop=(o == PASSES - 1),
+                    )
+            rows = keep.tile([P, PACK, J], F32, name="y_rows%d" % g)
+            stored = out_0[g * SPAN : (g + 1) * SPAN, :].rearrange("(p t) j -> p t j", t=PACK)
+            for t in range(PACK):
+                nc.vector.tensor_sub(out=rows[:, t, :], in0=banks[t][:], in1=label_rows[2 * g + t // 2][:, t % 2, :])
+                nc.sync.dma_start(out=stored[:, t, :], in_=rows[:, t, :])
+            y_rows.append(rows)
+            grouped = keep.tile([P, PACK * J], BF16, name="y_grouped%d" % g, align_bytes=64)
+            shared_interleave(nc, grouped[:], rows, Y_SCALAR_COLS[g])
+            y_grouped.append(grouped)
+
+        for g in range(GROUPS):
+            codes = keep.tile([P, J], U32, name="y_codes%d" % g, tag="label_rows1_%d" % (1 - g), align_bytes=64)
+            nc.vector.quantize_mx(out=codes[:].bitcast(FP8X4), scales=y_planes[:, g, :], in_=y_grouped[g][:])
+            nc.sync.dma_start(
+                out=out_1[g].rearrange("p c t -> p (c t)").bitcast(I32), in_=codes[:].bitcast(I32)
+            )
+        for q in range(QUADS):
+            nc.scalar.dma_start(
+                out=out_2[:, 4 * q : 4 * q + 4, :].rearrange("g r c -> r g c").bitcast(I32),
+                in_=y_planes[32 * q : 32 * q + 4, :, :].bitcast(I32),
+            )

@@ -56,18 +56,17 @@ def tile_picked_znceg_sq_po_kernel(tc, x_words, x_scales, hT, label, offs, out_0
                 in_=x_words[o].rearrange("p c t -> p (c t)")[:, PACK * lo : PACK * hi].bitcast(I32),
             )
 
-        def load_scales(o):
+        def load_scales(o, queue):
             for r in range(4):
-                nc.sync.dma_start(
+                queue.dma_start(
                     out=scale_table[4 * o + r : P : 32, :].bitcast(I32),
                     in_=x_scales[o, r:16:4, :].bitcast(I32),
                 )
 
         load_words(0, 0, T // 4)
-        load_scales(0)
-        load_words(0, T // 4, T // 2)
-        load_scales(1)
-        load_words(0, T // 2, T)
+        load_scales(0, nc.gpsimd)
+        load_scales(1, nc.sync)
+        load_words(0, T // 4, T)
         load_words(1, 0, T)
         h_rows = []
         for o in range(PASSES):
@@ -147,7 +146,10 @@ def tile_picked_znceg_sq_po_kernel(tc, x_words, x_scales, hT, label, offs, out_0
             stored = out_0[g * SPAN : (g + 1) * SPAN, :].rearrange("(p t) j -> p t j", t=PACK)
             for t in range(PACK):
                 nc.vector.tensor_sub(out=rows[:, t, :], in0=banks[t][:], in1=label_rows[2 * g + t // 2][:, t % 2, :])
-                nc.sync.dma_start(out=stored[:, t, :], in_=rows[:, t, :])
+                if g == GROUPS - 1 and t >= 2:
+                    nc.sync.dma_start(out=stored[:, t, :], in_=rows[:, t, :])
+                elif t % 2 == 1:
+                    nc.sync.dma_start(out=stored[:, t - 1 : t + 1, :], in_=rows[:, t - 1 : t + 1, :])
             y_rows.append(rows)
             grouped = keep.tile([P, PACK * J], BF16, name="y_grouped%d" % g, align_bytes=64)
             shared_interleave(nc, grouped[:], rows, Y_SCALAR_COLS[g])

@@ -47,6 +47,8 @@ def tile_picked_znceg_sq_po_kernel(tc, x_words, x_scales, hT, label, offs, out_0
 
         scale_table = keep.tile([P, T], U8, name="scale_table", align_bytes=64)
         nc.vector.memset(scale_table[:].bitcast(I32), 0)
+        x_planes = keep.tile([P, S], U8, name="x_planes", align_bytes=64)
+        nc.vector.memset(x_planes[:].bitcast(I32), 0)
 
         word_table = [keep.tile([P, T], U32, name="word_table%d" % o, align_bytes=64) for o in range(PASSES)]
 
@@ -56,18 +58,30 @@ def tile_picked_znceg_sq_po_kernel(tc, x_words, x_scales, hT, label, offs, out_0
                 in_=x_words[o].rearrange("p c t -> p (c t)")[:, PACK * lo : PACK * hi].bitcast(I32),
             )
 
-        def load_scales(o, queue):
+        load_words(0, 0, T // 4)
+        nc.sync.dma_start(
+            out=scale_table[0:P:4, :].bitcast(I32), in_=x_scales.rearrange("o q c -> (o q) c").bitcast(I32)
+        )
+        load_words(0, T // 4, T)
+        load_words(1, 0, 7 * T // 8)
+
+        picked_scales = keep.tile([P, S], U8, name="picked_scales", align_bytes=64)
+        nc.vector.tensor_copy(picked_scales[:], scale_table[:].indirect(offsets[:]))
+        dealt_scales = keep.tile([P, S], U8, name="dealt_scales", align_bytes=64)
+        nc.vector.tensor_copy(
+            out=dealt_scales[:].rearrange("p (g t c i) -> p g c t i", g=GROUPS, t=PACK, i=16),
+            in_=picked_scales[:].rearrange("p (g c i t) -> p g c t i", g=GROUPS, t=PACK, i=16),
+        )
+
+        def move_scales(o):
             for r in range(4):
-                queue.dma_start(
-                    out=scale_table[4 * o + r : P : 32, :].bitcast(I32),
-                    in_=x_scales[o, r:16:4, :].bitcast(I32),
+                nc.sync.dma_start(
+                    out=x_planes[4 * o + r : P : 32, :].bitcast(I32),
+                    in_=dealt_scales[64 * o + 4 * r : 64 * o + 64 : 16, :].bitcast(I32),
                 )
 
-        load_words(0, 0, T // 4)
-        load_scales(0, nc.gpsimd)
-        load_scales(1, nc.sync)
-        load_words(0, T // 4, T)
-        load_words(1, 0, T)
+        move_scales(0)
+        load_words(1, 7 * T // 8, T)
         h_rows = []
         for o in range(PASSES):
             rows = keep.tile([P, PACK, J], F32, name="h_rows%d" % o, align_bytes=64)
@@ -75,6 +89,8 @@ def tile_picked_znceg_sq_po_kernel(tc, x_words, x_scales, hT, label, offs, out_0
                 out=rows[:], in_=hT[o * SPAN : (o + 1) * SPAN, :].rearrange("(p t) j -> p t j", t=PACK)
             )
             h_rows.append(rows)
+            if o == 0:
+                move_scales(1)
         label_rows = []
         for g in range(GROUPS):
             dealt = label[g * SPAN : (g + 1) * SPAN, :].rearrange("(p t) j -> p t j", t=PACK)
@@ -83,17 +99,10 @@ def tile_picked_znceg_sq_po_kernel(tc, x_words, x_scales, hT, label, offs, out_0
                 nc.sync.dma_start(out=rows[:], in_=dealt[:, 2 * u : 2 * u + 2, :])
                 label_rows.append(rows)
 
-        picked_scales = keep.tile([P, S], U8, name="picked_scales", align_bytes=64)
-        nc.vector.tensor_copy(picked_scales[:], scale_table[:].indirect(offsets[:]))
         picked_words = []
         x_codes = []
         for o in range(PASSES):
             picked_words.append(keep.tile([P, S], U32, name="picked_words%d" % o, align_bytes=64))
-        x_planes = keep.tile([P, S], U8, name="x_planes", align_bytes=64)
-        nc.vector.tensor_copy(
-            out=x_planes[:].rearrange("p (g t c i) -> p g c t i", g=GROUPS, t=PACK, i=16),
-            in_=picked_scales[:].rearrange("p (g c i t) -> p g c t i", g=GROUPS, t=PACK, i=16),
-        )
 
         def deal_words(o, tag):
             x_codes.append(keep.tile([P, S], U32, name="x_codes%d" % o, tag=tag, align_bytes=64))
@@ -127,11 +136,9 @@ def tile_picked_znceg_sq_po_kernel(tc, x_words, x_scales, hT, label, offs, out_0
         y_grouped = []
         for g in range(GROUPS):
             banks = [psum.tile([P, J], F32, name="bank%d" % t) for t in range(PACK)]
-            order = [(o, t) for o in range(PASSES) for t in range(PACK)]
-            if g > 0:
-                order = sorted(order, key=lambda pair: pair[1])
-            for o, t in order:
-                if True:
+            for t in range(PACK):
+                order = (1, 0) if (g, t) == (0, PACK - 1) else (0, 1)
+                for o in order:
                     cols = slice(g * SPAN + t * P, g * SPAN + (t + 1) * P)
                     nc.tensor.matmul_mx(
                         out=banks[t][:],
@@ -139,8 +146,8 @@ def tile_picked_znceg_sq_po_kernel(tc, x_words, x_scales, hT, label, offs, out_0
                         lhsT_scale=x_planes[4 * o : P, cols],
                         rhs=h_codes[o][:].bitcast(FP8X4),
                         rhs_scale=h_planes[o][:],
-                        start=(o == 0),
-                        stop=(o == PASSES - 1),
+                        start=(o == order[0]),
+                        stop=(o == order[-1]),
                     )
             rows = keep.tile([P, PACK, J], F32, name="y_rows%d" % g)
             stored = out_0[g * SPAN : (g + 1) * SPAN, :].rearrange("(p t) j -> p t j", t=PACK)

@@ -43,11 +43,10 @@ def tile_picked_znceg_sq_po_kernel(tc, x_words, x_scales, hT, label, offs, out_0
         psum = ctx.enter_context(tc.psum_pool(name="psum", bufs=1))
 
         offsets = keep.tile([P, S // 16], U16, name="offsets")
-        nc.sync.dma_start(offsets[:], offs)
 
         scale_table = keep.tile([P, T], U8, name="scale_table", align_bytes=64)
         nc.vector.memset(scale_table[:].bitcast(I32), 0)
-        x_planes = keep.tile([P, S], U8, name="x_planes", align_bytes=64)
+        x_planes = keep.tile([P, PASSES * S], U8, name="x_planes", align_bytes=64)
         nc.vector.memset(x_planes[:].bitcast(I32), 0)
 
         word_table = [keep.tile([P, T], U32, name="word_table%d" % o, align_bytes=64) for o in range(PASSES)]
@@ -59,11 +58,12 @@ def tile_picked_znceg_sq_po_kernel(tc, x_words, x_scales, hT, label, offs, out_0
             )
 
         load_words(0, 0, T // 4)
+        nc.sync.dma_start(offsets[:], offs)
         nc.sync.dma_start(
             out=scale_table[0:P:4, :].bitcast(I32), in_=x_scales.rearrange("o q c -> (o q) c").bitcast(I32)
         )
         load_words(0, T // 4, T)
-        load_words(1, 0, 7 * T // 8)
+        load_words(1, 0, T)
 
         picked_scales = keep.tile([P, S], U8, name="picked_scales", align_bytes=64)
         nc.vector.tensor_copy(picked_scales[:], scale_table[:].indirect(offsets[:]))
@@ -76,12 +76,10 @@ def tile_picked_znceg_sq_po_kernel(tc, x_words, x_scales, hT, label, offs, out_0
         def move_scales(o):
             for r in range(4):
                 nc.sync.dma_start(
-                    out=x_planes[4 * o + r : P : 32, :].bitcast(I32),
+                    out=x_planes[r:P:32, o * S : (o + 1) * S].bitcast(I32),
                     in_=dealt_scales[64 * o + 4 * r : 64 * o + 64 : 16, :].bitcast(I32),
                 )
 
-        move_scales(0)
-        load_words(1, 7 * T // 8, T)
         h_rows = []
         for o in range(PASSES):
             rows = keep.tile([P, PACK, J], F32, name="h_rows%d" % o, align_bytes=64)
@@ -89,8 +87,7 @@ def tile_picked_znceg_sq_po_kernel(tc, x_words, x_scales, hT, label, offs, out_0
                 out=rows[:], in_=hT[o * SPAN : (o + 1) * SPAN, :].rearrange("(p t) j -> p t j", t=PACK)
             )
             h_rows.append(rows)
-            if o == 0:
-                move_scales(1)
+            move_scales(o)
         label_rows = []
         for g in range(GROUPS):
             dealt = label[g * SPAN : (g + 1) * SPAN, :].rearrange("(p t) j -> p t j", t=PACK)
@@ -100,21 +97,25 @@ def tile_picked_znceg_sq_po_kernel(tc, x_words, x_scales, hT, label, offs, out_0
                 label_rows.append(rows)
 
         picked_words = []
-        x_codes = []
+        x_codes = {}
         for o in range(PASSES):
             picked_words.append(keep.tile([P, S], U32, name="picked_words%d" % o, align_bytes=64))
 
-        def deal_words(o, tag):
-            x_codes.append(keep.tile([P, S], U32, name="x_codes%d" % o, tag=tag, align_bytes=64))
+        def deal_words(o, groups, tag):
+            n = len(groups)
+            codes = keep.tile([P, n * SPAN], U32, name="x_codes%d_%d" % (o, groups[0]), tag=tag, align_bytes=64)
+            picked = picked_words[o][:, groups[0] * SPAN : (groups[0] + n) * SPAN]
             nc.vector.tensor_copy(
-                out=x_codes[o][:].bitcast(I32).rearrange("p (g t c i) -> p g c t i", g=GROUPS, t=PACK, i=4),
-                in_=picked_words[o][:].bitcast(I32).rearrange("p (g c i t) -> p g c t i", g=GROUPS, t=PACK, i=4),
+                out=codes[:].bitcast(I32).rearrange("p (g t c i) -> p g c t i", g=n, t=PACK, i=4),
+                in_=picked.bitcast(I32).rearrange("p (g c i t) -> p g c t i", g=n, t=PACK, i=4),
             )
+            for a, g in enumerate(groups):
+                x_codes[(o, g)] = codes[:, a * SPAN : (a + 1) * SPAN]
 
         for o in range(PASSES):
             nc.vector.tensor_copy(picked_words[o][:], word_table[o][:].indirect(offsets[:]))
             if o == 0:
-                deal_words(0, "x_codes0")
+                deal_words(0, (0, 1), "x_codes0")
 
         h_codes = []
         h_planes = []
@@ -128,8 +129,7 @@ def tile_picked_znceg_sq_po_kernel(tc, x_words, x_scales, hT, label, offs, out_0
             nc.vector.quantize_mx(out=codes[:].bitcast(FP8X4), scales=plane[:], in_=grouped)
             h_codes.append(codes)
             h_planes.append(plane)
-            if o == 0:
-                deal_words(1, "h_rows0")
+            deal_words(1, (o,), "h_rows%d" % o)
 
         y_planes = keep.tile([P, GROUPS, J], U8, name="y_planes", align_bytes=64)
         y_rows = []
@@ -137,13 +137,13 @@ def tile_picked_znceg_sq_po_kernel(tc, x_words, x_scales, hT, label, offs, out_0
         for g in range(GROUPS):
             banks = [psum.tile([P, J], F32, name="bank%d" % t) for t in range(PACK)]
             for t in range(PACK):
-                order = (1, 0) if (g, t) == (0, PACK - 1) else (0, 1)
+                order = (0, 1)
                 for o in order:
-                    cols = slice(g * SPAN + t * P, g * SPAN + (t + 1) * P)
+                    cols = slice(o * S + g * SPAN + t * P, o * S + g * SPAN + (t + 1) * P)
                     nc.tensor.matmul_mx(
                         out=banks[t][:],
-                        lhsT=x_codes[o][:, cols].bitcast(FP8X4),
-                        lhsT_scale=x_planes[4 * o : P, cols],
+                        lhsT=x_codes[(o, g)][:, t * P : (t + 1) * P].bitcast(FP8X4),
+                        lhsT_scale=x_planes[:, cols],
                         rhs=h_codes[o][:].bitcast(FP8X4),
                         rhs_scale=h_planes[o][:],
                         start=(o == order[0]),
@@ -152,8 +152,9 @@ def tile_picked_znceg_sq_po_kernel(tc, x_words, x_scales, hT, label, offs, out_0
             rows = keep.tile([P, PACK, J], F32, name="y_rows%d" % g)
             stored = out_0[g * SPAN : (g + 1) * SPAN, :].rearrange("(p t) j -> p t j", t=PACK)
             for t in range(PACK):
-                nc.vector.tensor_sub(out=rows[:, t, :], in0=banks[t][:], in1=label_rows[2 * g + t // 2][:, t % 2, :])
-                if g == GROUPS - 1 and t >= 2:
+                target = label_rows[2 * g + t // 2][:, t % 2, :]
+                nc.vector.tensor_sub(out=rows[:, t, :], in0=banks[t][:], in1=target)
+                if t // 2 == g:
                     nc.sync.dma_start(out=stored[:, t, :], in_=rows[:, t, :])
                 elif t % 2 == 1:
                     nc.sync.dma_start(out=stored[:, t - 1 : t + 1, :], in_=rows[:, t - 1 : t + 1, :])

@@ -19,8 +19,10 @@ SPAN = P * PACK
 PASSES = K // SPAN
 GROUPS = S // SPAN
 QUADS = 4
-H_SCALAR_COLS = (192, 192)
-Y_SCALAR_COLS = (512, 192)
+H1_SCALAR_COLS = 176
+Y_SCALAR_COLS = 128
+WORDS_BEFORE_MOVES = 3 * T // 4
+HALF = J // 2
 
 
 def interleave(copy, grouped, rows, lo, hi):
@@ -28,12 +30,6 @@ def interleave(copy, grouped, rows, lo, hi):
         out=grouped[:, PACK * lo : PACK * hi].rearrange("p (c i t) -> p c t i", i=4, t=PACK),
         in_=rows[:, :, lo:hi].rearrange("p t (c i) -> p c t i", i=4),
     )
-
-
-def shared_interleave(nc, grouped, rows, scalar_cols):
-    interleave(nc.scalar.copy, grouped, rows, J - scalar_cols, J)
-    if scalar_cols < J:
-        interleave(nc.vector.tensor_copy, grouped, rows, 0, J - scalar_cols)
 
 
 def tile_picked_znceg_sq_po_kernel(tc, x_words, x_scales, hT, label, offs, out_0, out_1, out_2):
@@ -57,118 +53,158 @@ def tile_picked_znceg_sq_po_kernel(tc, x_words, x_scales, hT, label, offs, out_0
                 in_=x_words[o].rearrange("p c t -> p (c t)")[:, PACK * lo : PACK * hi].bitcast(I32),
             )
 
-        load_words(0, 0, T // 4)
-        nc.sync.dma_start(offsets[:], offs)
-        nc.sync.dma_start(
-            out=scale_table[0:P:4, :].bitcast(I32), in_=x_scales.rearrange("o q c -> (o q) c").bitcast(I32)
-        )
-        load_words(0, T // 4, T)
-        load_words(1, 0, T)
+        def load_rows(name, source, block, t_lo, t_hi, lo, hi):
+            rows = keep.tile([P, t_hi - t_lo, hi - lo], F32, name=name, align_bytes=64)
+            dealt = source[block * SPAN : (block + 1) * SPAN, :].rearrange("(p t) j -> p t j", t=PACK)
+            nc.sync.dma_start(out=rows[:], in_=dealt[:, t_lo:t_hi, lo:hi])
+            return rows
 
         picked_scales = keep.tile([P, S], U8, name="picked_scales", align_bytes=64)
-        nc.vector.tensor_copy(picked_scales[:], scale_table[:].indirect(offsets[:]))
         dealt_scales = keep.tile([P, S], U8, name="dealt_scales", align_bytes=64)
-        nc.vector.tensor_copy(
-            out=dealt_scales[:].rearrange("p (g t c i) -> p g c t i", g=GROUPS, t=PACK, i=16),
-            in_=picked_scales[:].rearrange("p (g c i t) -> p g c t i", g=GROUPS, t=PACK, i=16),
-        )
 
-        def move_scales(o):
-            for r in range(4):
+        def load_scales():
+            nc.sync.dma_start(offsets[:], offs)
+            nc.sync.dma_start(
+                out=scale_table[0:P:4, :].bitcast(I32), in_=x_scales.rearrange("o q c -> q o c").bitcast(I32)
+            )
+            nc.vector.tensor_copy(picked_scales[:], scale_table[:].indirect(offsets[:]))
+            nc.vector.tensor_copy(
+                out=dealt_scales[:].rearrange("p (g t c i) -> p g c t i", g=GROUPS, t=PACK, i=16),
+                in_=picked_scales[:].rearrange("p (g c i t) -> p g c t i", g=GROUPS, t=PACK, i=16),
+            )
+
+        def move_scales():
+            for q in range(QUADS):
                 nc.sync.dma_start(
-                    out=x_planes[r:P:32, o * S : (o + 1) * S].bitcast(I32),
-                    in_=dealt_scales[64 * o + 4 * r : 64 * o + 64 : 16, :].bitcast(I32),
+                    out=x_planes[32 * q : 32 * q + 4, :].bitcast(I32),
+                    in_=dealt_scales[32 * q : 32 * q + 32 : 4, :].bitcast(I32),
                 )
 
-        h_rows = []
-        for o in range(PASSES):
-            rows = keep.tile([P, PACK, J], F32, name="h_rows%d" % o, align_bytes=64)
-            nc.sync.dma_start(
-                out=rows[:], in_=hT[o * SPAN : (o + 1) * SPAN, :].rearrange("(p t) j -> p t j", t=PACK)
-            )
-            h_rows.append(rows)
-            move_scales(o)
-        label_rows = []
-        for g in range(GROUPS):
-            dealt = label[g * SPAN : (g + 1) * SPAN, :].rearrange("(p t) j -> p t j", t=PACK)
-            for u in range(2):
-                rows = keep.tile([P, 2, J], F32, name="label_rows%d_%d" % (g, u), align_bytes=64)
-                nc.sync.dma_start(out=rows[:], in_=dealt[:, 2 * u : 2 * u + 2, :])
-                label_rows.append(rows)
+        h0 = load_rows("h0", hT, 0, 0, PACK, 0, J)
+        load_scales()
+        load_words(0, 0, T)
+        load_words(1, 0, WORDS_BEFORE_MOVES)
+        move_scales()
+        load_words(1, WORDS_BEFORE_MOVES, T)
+        h1a = load_rows("h1a", hT, 1, 0, PACK, 0, HALF)
+        h1b = load_rows("h1b", hT, 1, 0, PACK, HALF, J)
+        label_pairs = [
+            [load_rows("label%d_%d" % (g, u), label, g, 2 * u, 2 * u + 2, 0, J) for u in range(2)]
+            for g in range(GROUPS)
+        ]
 
-        picked_words = []
+        def target(g, t):
+            return label_pairs[g][t // 2][:, t % 2, :]
+
+        h_codes = [keep.tile([P, J], U32, name="h_codes%d" % o, align_bytes=64) for o in range(PASSES)]
+        h_planes = [keep.tile([P, J], U8, name="h_plane%d" % o, align_bytes=64) for o in range(PASSES)]
+
+        def round_h(grouped, rows, scalar_cols):
+            width = rows.shape[2]
+            interleave(nc.scalar.copy, grouped, rows, width - scalar_cols, width)
+            if scalar_cols < width:
+                interleave(nc.vector.tensor_copy, grouped, rows, 0, width - scalar_cols)
+
+        def quantize_h(o, grouped, lo, hi):
+            nc.vector.quantize_mx(
+                out=h_codes[o][:, lo:hi].bitcast(FP8X4), scales=h_planes[o][:, lo:hi], in_=grouped
+            )
+
         x_codes = {}
-        for o in range(PASSES):
-            picked_words.append(keep.tile([P, S], U32, name="picked_words%d" % o, align_bytes=64))
 
-        def deal_words(o, groups, tag):
-            n = len(groups)
-            codes = keep.tile([P, n * SPAN], U32, name="x_codes%d_%d" % (o, groups[0]), tag=tag, align_bytes=64)
-            picked = picked_words[o][:, groups[0] * SPAN : (groups[0] + n) * SPAN]
+        def gather_words(o, g):
+            codes = keep.tile([P, SPAN], U32, name="x_codes%d_%d" % (o, g), align_bytes=64)
             nc.vector.tensor_copy(
-                out=codes[:].bitcast(I32).rearrange("p (g t c i) -> p g c t i", g=n, t=PACK, i=4),
-                in_=picked.bitcast(I32).rearrange("p (g c i t) -> p g c t i", g=n, t=PACK, i=4),
+                codes[:].rearrange("p (t m) -> p m t", t=PACK),
+                word_table[o][:].indirect(offsets[:, g * (SPAN // 16) : (g + 1) * (SPAN // 16)]),
             )
-            for a, g in enumerate(groups):
-                x_codes[(o, g)] = codes[:, a * SPAN : (a + 1) * SPAN]
+            x_codes[(o, g)] = codes
 
-        for o in range(PASSES):
-            nc.vector.tensor_copy(picked_words[o][:], word_table[o][:].indirect(offsets[:]))
-            if o == 0:
-                deal_words(0, (0, 1), "x_codes0")
+        banks = [
+            [psum.tile([P, J], F32, name="bank%d_%d" % (g, t)) for t in range(PACK)] for g in range(GROUPS)
+        ]
 
-        h_codes = []
-        h_planes = []
-        h_grouped = keep.tile([P, PACK * (J + H_SCALAR_COLS[1])], BF16, name="h_grouped", align_bytes=64)
+        def multiply(o, g, t):
+            cols = slice(o * S + g * SPAN + t * P, o * S + g * SPAN + (t + 1) * P)
+            nc.tensor.matmul_mx(
+                out=banks[g][t][:],
+                lhsT=x_codes[(o, g)][:, t * P : (t + 1) * P].bitcast(FP8X4),
+                lhsT_scale=x_planes[:, cols],
+                rhs=h_codes[o][:].bitcast(FP8X4),
+                rhs_scale=h_planes[o][:],
+                start=(o == 0),
+                stop=(o == PASSES - 1),
+            )
+
+        h0_grouped = keep.tile([P, PACK * J], BF16, name="h0_grouped", align_bytes=64)
+        round_h(h0_grouped[:], h0, J)
+        quantize_h(0, h0_grouped[:], 0, J)
         for o in range(PASSES):
-            first = o * PACK * H_SCALAR_COLS[1]
-            grouped = h_grouped[:, first : first + PACK * J]
-            shared_interleave(nc, grouped, h_rows[o], H_SCALAR_COLS[o])
-            codes = keep.tile([P, J], U32, name="h_codes%d" % o, align_bytes=64)
-            plane = keep.tile([P, J], U8, name="h_plane%d" % o, align_bytes=64)
-            nc.vector.quantize_mx(out=codes[:].bitcast(FP8X4), scales=plane[:], in_=grouped)
-            h_codes.append(codes)
-            h_planes.append(plane)
-            deal_words(1, (o,), "h_rows%d" % o)
+            for g in range(GROUPS):
+                gather_words(o, g)
+        h1_grouped = keep.tile([P, PACK * (HALF + H1_SCALAR_COLS)], BF16, name="h1_grouped", align_bytes=64)
+        h1a_grouped = h1_grouped[:, : PACK * HALF]
+        h1b_grouped = h1_grouped[:, PACK * H1_SCALAR_COLS :]
+        round_h(h1a_grouped, h1a, HALF)
+        quantize_h(1, h1a_grouped, 0, HALF)
+        round_h(h1b_grouped, h1b, H1_SCALAR_COLS)
+        quantize_h(1, h1b_grouped, HALF, J)
+        for o in range(PASSES):
+            for g in range(GROUPS):
+                for t in range(PACK):
+                    multiply(o, g, t)
 
         y_planes = keep.tile([P, GROUPS, J], U8, name="y_planes", align_bytes=64)
-        y_rows = []
-        y_grouped = []
-        for g in range(GROUPS):
-            banks = [psum.tile([P, J], F32, name="bank%d" % t) for t in range(PACK)]
-            for t in range(PACK):
-                order = (0, 1)
-                for o in order:
-                    cols = slice(o * S + g * SPAN + t * P, o * S + g * SPAN + (t + 1) * P)
-                    nc.tensor.matmul_mx(
-                        out=banks[t][:],
-                        lhsT=x_codes[(o, g)][:, t * P : (t + 1) * P].bitcast(FP8X4),
-                        lhsT_scale=x_planes[:, cols],
-                        rhs=h_codes[o][:].bitcast(FP8X4),
-                        rhs_scale=h_planes[o][:],
-                        start=(o == order[0]),
-                        stop=(o == order[-1]),
-                    )
-            rows = keep.tile([P, PACK, J], F32, name="y_rows%d" % g)
+        y_rows = [keep.tile([P, PACK, J], F32, name="y_rows%d" % g) for g in range(GROUPS)]
+        y_grouped = [
+            keep.tile([P, PACK * J], BF16, name="y_grouped%d" % g, align_bytes=64) for g in range(GROUPS)
+        ]
+        y_codes = [keep.tile([P, J], U32, name="y_codes%d" % g, align_bytes=64) for g in range(GROUPS)]
+
+        def subtract(g, t, lo, hi):
+            nc.vector.tensor_sub(out=y_rows[g][:, t, lo:hi], in0=banks[g][t][:, lo:hi], in1=target(g, t)[:, lo:hi])
+
+        def store_rows(g, lo, hi):
             stored = out_0[g * SPAN : (g + 1) * SPAN, :].rearrange("(p t) j -> p t j", t=PACK)
-            for t in range(PACK):
-                target = label_rows[2 * g + t // 2][:, t % 2, :]
-                nc.vector.tensor_sub(out=rows[:, t, :], in0=banks[t][:], in1=target)
-                if t // 2 == g:
-                    nc.sync.dma_start(out=stored[:, t, :], in_=rows[:, t, :])
-                elif t % 2 == 1:
-                    nc.sync.dma_start(out=stored[:, t - 1 : t + 1, :], in_=rows[:, t - 1 : t + 1, :])
-            y_rows.append(rows)
-            grouped = keep.tile([P, PACK * J], BF16, name="y_grouped%d" % g, align_bytes=64)
-            shared_interleave(nc, grouped[:], rows, Y_SCALAR_COLS[g])
-            y_grouped.append(grouped)
+            nc.sync.dma_start(out=stored[:, lo:hi, :], in_=y_rows[g][:, lo:hi, :])
+
+        def round_y(copy, g, lo, hi):
+            interleave(copy, y_grouped[g][:], y_rows[g], lo, hi)
+
+        def quantize_y(g, lo, hi):
+            nc.vector.quantize_mx(
+                out=y_codes[g][:, lo:hi].bitcast(FP8X4),
+                scales=y_planes[:, g, lo:hi],
+                in_=y_grouped[g][:, PACK * lo : PACK * hi],
+            )
+
+        def store_codes(g):
+            nc.sync.dma_start(
+                out=out_1[g].rearrange("p c t -> p (c t)").bitcast(I32), in_=y_codes[g][:].bitcast(I32)
+            )
 
         for g in range(GROUPS):
-            codes = keep.tile([P, J], U32, name="y_codes%d" % g, tag="label_rows1_%d" % (1 - g), align_bytes=64)
-            nc.vector.quantize_mx(out=codes[:].bitcast(FP8X4), scales=y_planes[:, g, :], in_=y_grouped[g][:])
-            nc.sync.dma_start(
-                out=out_1[g].rearrange("p c t -> p (c t)").bitcast(I32), in_=codes[:].bitcast(I32)
-            )
+            for t in range(2):
+                subtract(g, t, 0, J)
+                if g == 0:
+                    store_rows(g, t, t + 1)
+            if g == 1:
+                store_rows(g, 0, 2)
+            for t in range(2, PACK):
+                subtract(g, t, 0, HALF)
+            round_y(nc.scalar.copy, g, 0, HALF)
+            for t in range(2, PACK):
+                subtract(g, t, HALF, J)
+            store_rows(g, 2, PACK)
+            if g == 0:
+                round_y(nc.scalar.copy, g, HALF, J)
+        quantize_y(0, 0, J)
+        store_codes(0)
+        round_y(nc.scalar.copy, 1, J - Y_SCALAR_COLS, J)
+        round_y(nc.vector.tensor_copy, 1, HALF, J - Y_SCALAR_COLS)
+        quantize_y(1, 0, HALF)
+        quantize_y(1, HALF, J)
+        store_codes(1)
         for q in range(QUADS):
             nc.scalar.dma_start(
                 out=out_2[:, 4 * q : 4 * q + 4, :].rearrange("g r c -> r g c").bitcast(I32),

@@ -65,7 +65,7 @@ def tile_picked_znceg_sq_po_kernel(tc, x_words, x_scales, hT, label, offs, out_0
         def load_scales():
             nc.sync.dma_start(offsets[:], offs)
             nc.sync.dma_start(
-                out=scale_table[0:P:4, :].bitcast(I32), in_=x_scales.rearrange("o q c -> q o c").bitcast(I32)
+                out=scale_table[0:P:4, :].bitcast(I32), in_=x_scales.rearrange("o q c -> (o q) c").bitcast(I32)
             )
             nc.vector.tensor_copy(picked_scales[:], scale_table[:].indirect(offsets[:]))
             nc.vector.tensor_copy(
@@ -73,21 +73,22 @@ def tile_picked_znceg_sq_po_kernel(tc, x_words, x_scales, hT, label, offs, out_0
                 in_=picked_scales[:].rearrange("p (g c i t) -> p g c t i", g=GROUPS, t=PACK, i=16),
             )
 
-        def move_scales():
-            for q in range(QUADS):
+        def move_scales(o):
+            for r in range(4):
                 nc.sync.dma_start(
-                    out=x_planes[32 * q : 32 * q + 4, :].bitcast(I32),
-                    in_=dealt_scales[32 * q : 32 * q + 32 : 4, :].bitcast(I32),
+                    out=x_planes[r:P:32, o * S : (o + 1) * S].bitcast(I32),
+                    in_=dealt_scales[64 * o + 4 * r : 64 * o + 64 : 16, :].bitcast(I32),
                 )
 
         h0 = load_rows("h0", hT, 0, 0, PACK, 0, J)
         load_scales()
         load_words(0, 0, T)
         load_words(1, 0, WORDS_BEFORE_MOVES)
-        move_scales()
+        move_scales(0)
         load_words(1, WORDS_BEFORE_MOVES, T)
         h1a = load_rows("h1a", hT, 1, 0, PACK, 0, HALF)
         h1b = load_rows("h1b", hT, 1, 0, PACK, HALF, J)
+        move_scales(1)
         label_pairs = [
             [load_rows("label%d_%d" % (g, u), label, g, 2 * u, 2 * u + 2, 0, J) for u in range(2)]
             for g in range(GROUPS)

@@ -20,8 +20,7 @@ PASSES = K // SPAN
 GROUPS = S // SPAN
 QUADS = 4
 H1_SCALAR_COLS = 176
-Y_SCALAR_COLS = 128
-WORDS_BEFORE_MOVES = 3 * T // 4
+Y_SCALAR_COLS = 64
 HALF = J // 2
 
 
@@ -83,9 +82,8 @@ def tile_picked_znceg_sq_po_kernel(tc, x_words, x_scales, hT, label, offs, out_0
         h0 = load_rows("h0", hT, 0, 0, PACK, 0, J)
         load_scales()
         load_words(0, 0, T)
-        load_words(1, 0, WORDS_BEFORE_MOVES)
+        load_words(1, 0, T)
         move_scales(0)
-        load_words(1, WORDS_BEFORE_MOVES, T)
         h1a = load_rows("h1a", hT, 1, 0, PACK, 0, HALF)
         h1b = load_rows("h1b", hT, 1, 0, PACK, HALF, J)
         move_scales(1)
@@ -93,9 +91,6 @@ def tile_picked_znceg_sq_po_kernel(tc, x_words, x_scales, hT, label, offs, out_0
             [load_rows("label%d_%d" % (g, u), label, g, 2 * u, 2 * u + 2, 0, J) for u in range(2)]
             for g in range(GROUPS)
         ]
-
-        def target(g, t):
-            return label_pairs[g][t // 2][:, t % 2, :]
 
         h_codes = [keep.tile([P, J], U32, name="h_codes%d" % o, align_bytes=64) for o in range(PASSES)]
         h_planes = [keep.tile([P, J], U8, name="h_plane%d" % o, align_bytes=64) for o in range(PASSES)]
@@ -121,18 +116,22 @@ def tile_picked_znceg_sq_po_kernel(tc, x_words, x_scales, hT, label, offs, out_0
             )
             x_codes[(o, g)] = codes
 
-        banks = [
-            [psum.tile([P, J], F32, name="bank%d_%d" % (g, t)) for t in range(PACK)] for g in range(GROUPS)
-        ]
+        banks = {
+            (g, u, v): psum.tile([P, 2, HALF], F32, name="bank%d_%d_%d" % (g, u, v))
+            for g in range(GROUPS)
+            for u in range(2)
+            for v in range(2)
+        }
 
-        def multiply(o, g, t):
+        def multiply(o, g, t, v):
             cols = slice(o * S + g * SPAN + t * P, o * S + g * SPAN + (t + 1) * P)
+            half = slice(v * HALF, (v + 1) * HALF)
             nc.tensor.matmul_mx(
-                out=banks[g][t][:],
+                out=banks[(g, t // 2, v)][:, t % 2, :],
                 lhsT=x_codes[(o, g)][:, t * P : (t + 1) * P].bitcast(FP8X4),
                 lhsT_scale=x_planes[:, cols],
-                rhs=h_codes[o][:].bitcast(FP8X4),
-                rhs_scale=h_planes[o][:],
+                rhs=h_codes[o][:, half].bitcast(FP8X4),
+                rhs_scale=h_planes[o][:, half],
                 start=(o == 0),
                 stop=(o == PASSES - 1),
             )
@@ -150,10 +149,12 @@ def tile_picked_znceg_sq_po_kernel(tc, x_words, x_scales, hT, label, offs, out_0
         quantize_h(1, h1a_grouped, 0, HALF)
         round_h(h1b_grouped, h1b, H1_SCALAR_COLS)
         quantize_h(1, h1b_grouped, HALF, J)
-        for o in range(PASSES):
-            for g in range(GROUPS):
-                for t in range(PACK):
-                    multiply(o, g, t)
+        for g, u, v in banks:
+            multiply(0, g, 2 * u, v)
+        for g, u, v in banks:
+            multiply(1, g, 2 * u, v)
+            for o in range(PASSES):
+                multiply(o, g, 2 * u + 1, v)
 
         y_planes = keep.tile([P, GROUPS, J], U8, name="y_planes", align_bytes=64)
         y_rows = [keep.tile([P, PACK, J], F32, name="y_rows%d" % g) for g in range(GROUPS)]
@@ -162,8 +163,13 @@ def tile_picked_znceg_sq_po_kernel(tc, x_words, x_scales, hT, label, offs, out_0
         ]
         y_codes = [keep.tile([P, J], U32, name="y_codes%d" % g, align_bytes=64) for g in range(GROUPS)]
 
-        def subtract(g, t, lo, hi):
-            nc.vector.tensor_sub(out=y_rows[g][:, t, lo:hi], in0=banks[g][t][:, lo:hi], in1=target(g, t)[:, lo:hi])
+        def subtract(g, u, v):
+            half = slice(v * HALF, (v + 1) * HALF)
+            nc.vector.tensor_sub(
+                out=y_rows[g][:, 2 * u : 2 * u + 2, half],
+                in0=banks[(g, u, v)][:],
+                in1=label_pairs[g][u][:, :, half],
+            )
 
         def store_rows(g, lo, hi):
             stored = out_0[g * SPAN : (g + 1) * SPAN, :].rearrange("(p t) j -> p t j", t=PACK)
@@ -185,17 +191,12 @@ def tile_picked_znceg_sq_po_kernel(tc, x_words, x_scales, hT, label, offs, out_0
             )
 
         for g in range(GROUPS):
-            for t in range(2):
-                subtract(g, t, 0, J)
-                if g == 0:
-                    store_rows(g, t, t + 1)
-            if g == 1:
-                store_rows(g, 0, 2)
-            for t in range(2, PACK):
-                subtract(g, t, 0, HALF)
+            for v in range(2):
+                subtract(g, 0, v)
+            store_rows(g, 0, 2)
+            subtract(g, 1, 0)
             round_y(nc.scalar.copy, g, 0, HALF)
-            for t in range(2, PACK):
-                subtract(g, t, HALF, J)
+            subtract(g, 1, 1)
             store_rows(g, 2, PACK)
             if g == 0:
                 round_y(nc.scalar.copy, g, HALF, J)
@@ -206,8 +207,9 @@ def tile_picked_znceg_sq_po_kernel(tc, x_words, x_scales, hT, label, offs, out_0
         quantize_y(1, 0, HALF)
         quantize_y(1, HALF, J)
         store_codes(1)
-        for q in range(QUADS):
-            nc.scalar.dma_start(
-                out=out_2[:, 4 * q : 4 * q + 4, :].rearrange("g r c -> r g c").bitcast(I32),
-                in_=y_planes[32 * q : 32 * q + 4, :, :].bitcast(I32),
+        for r in range(4):
+            queue = nc.sync if r == 0 else nc.scalar
+            queue.dma_start(
+                out=out_2[:, r : 4 * QUADS : 4, :].rearrange("g q c -> q g c").bitcast(I32),
+                in_=y_planes[r:P:32, :, :].bitcast(I32),
             )

@@ -19,9 +19,11 @@ SPAN = P * PACK
 PASSES = K // SPAN
 GROUPS = S // SPAN
 QUADS = 4
-H1_SCALAR_COLS = 176
+H0_SCALAR_COLS = 208
+H1_SCALAR_COLS = (128, 96)
 Y_SCALAR_COLS = 64
 HALF = J // 2
+WARM_UPS = 3
 
 
 def interleave(copy, grouped, rows, lo, hi):
@@ -41,8 +43,9 @@ def tile_picked_znceg_sq_po_kernel(tc, x_words, x_scales, hT, label, offs, out_0
 
         scale_table = keep.tile([P, T], U8, name="scale_table", align_bytes=64)
         nc.vector.memset(scale_table[:].bitcast(I32), 0)
-        x_planes = keep.tile([P, PASSES * S], U8, name="x_planes", align_bytes=64)
-        nc.vector.memset(x_planes[:].bitcast(I32), 0)
+        x_planes = [keep.tile([P, S], U8, name="x_plane%d" % o, align_bytes=64) for o in range(PASSES)]
+        for plane in x_planes:
+            nc.vector.memset(plane[:].bitcast(I32), 0)
 
         word_table = [keep.tile([P, T], U32, name="word_table%d" % o, align_bytes=64) for o in range(PASSES)]
 
@@ -75,36 +78,29 @@ def tile_picked_znceg_sq_po_kernel(tc, x_words, x_scales, hT, label, offs, out_0
         def move_scales(o):
             for r in range(4):
                 nc.sync.dma_start(
-                    out=x_planes[r:P:32, o * S : (o + 1) * S].bitcast(I32),
+                    out=x_planes[o][r:P:32, :].bitcast(I32),
                     in_=dealt_scales[64 * o + 4 * r : 64 * o + 64 : 16, :].bitcast(I32),
                 )
 
-        h0 = load_rows("h0", hT, 0, 0, PACK, 0, J)
+        load_words(0, 0, T // 4)
         load_scales()
-        load_words(0, 0, T)
+        load_words(0, T // 4, T)
         load_words(1, 0, T)
         move_scales(0)
-        h1a = load_rows("h1a", hT, 1, 0, PACK, 0, HALF)
-        h1b = load_rows("h1b", hT, 1, 0, PACK, HALF, J)
+        h0 = load_rows("h0", hT, 0, 0, PACK, 0, J)
+        h1 = [load_rows("h1_%d" % v, hT, 1, 0, PACK, v * HALF, (v + 1) * HALF) for v in range(2)]
         move_scales(1)
         label_pairs = [
             [load_rows("label%d_%d" % (g, u), label, g, 2 * u, 2 * u + 2, 0, J) for u in range(2)]
             for g in range(GROUPS)
         ]
 
-        h_codes = [keep.tile([P, J], U32, name="h_codes%d" % o, align_bytes=64) for o in range(PASSES)]
-        h_planes = [keep.tile([P, J], U8, name="h_plane%d" % o, align_bytes=64) for o in range(PASSES)]
+        halves = [(o, v) for o in range(PASSES) for v in range(2)]
+        h_codes = {ov: keep.tile([P, HALF], U32, name="h_codes%d_%d" % ov, align_bytes=64) for ov in halves}
+        h_planes = {ov: keep.tile([P, HALF], U8, name="h_plane%d_%d" % ov, align_bytes=64) for ov in halves}
 
-        def round_h(grouped, rows, scalar_cols):
-            width = rows.shape[2]
-            interleave(nc.scalar.copy, grouped, rows, width - scalar_cols, width)
-            if scalar_cols < width:
-                interleave(nc.vector.tensor_copy, grouped, rows, 0, width - scalar_cols)
-
-        def quantize_h(o, grouped, lo, hi):
-            nc.vector.quantize_mx(
-                out=h_codes[o][:, lo:hi].bitcast(FP8X4), scales=h_planes[o][:, lo:hi], in_=grouped
-            )
+        def quantize_h(o, v, grouped):
+            nc.vector.quantize_mx(out=h_codes[(o, v)][:].bitcast(FP8X4), scales=h_planes[(o, v)][:], in_=grouped)
 
         x_codes = {}
 
@@ -116,45 +112,55 @@ def tile_picked_znceg_sq_po_kernel(tc, x_words, x_scales, hT, label, offs, out_0
             )
             x_codes[(o, g)] = codes
 
-        banks = {
-            (g, u, v): psum.tile([P, 2, HALF], F32, name="bank%d_%d_%d" % (g, u, v))
-            for g in range(GROUPS)
-            for u in range(2)
-            for v in range(2)
-        }
+        banks = {}
 
         def multiply(o, g, t, v):
-            cols = slice(o * S + g * SPAN + t * P, o * S + g * SPAN + (t + 1) * P)
-            half = slice(v * HALF, (v + 1) * HALF)
+            cols = slice(g * SPAN + t * P, g * SPAN + (t + 1) * P)
             nc.tensor.matmul_mx(
                 out=banks[(g, t // 2, v)][:, t % 2, :],
                 lhsT=x_codes[(o, g)][:, t * P : (t + 1) * P].bitcast(FP8X4),
-                lhsT_scale=x_planes[:, cols],
-                rhs=h_codes[o][:, half].bitcast(FP8X4),
-                rhs_scale=h_planes[o][:, half],
-                start=(o == 0),
-                stop=(o == PASSES - 1),
+                lhsT_scale=x_planes[o][:, cols],
+                rhs=h_codes[(o, v)][:].bitcast(FP8X4),
+                rhs_scale=h_planes[(o, v)][:],
+                start=(o == 0 and t % 2 == 0),
+                stop=(o == PASSES - 1 and t % 2 == 1),
             )
 
-        h0_grouped = keep.tile([P, PACK * J], BF16, name="h0_grouped", align_bytes=64)
-        round_h(h0_grouped[:], h0, J)
-        quantize_h(0, h0_grouped[:], 0, J)
         for o in range(PASSES):
             for g in range(GROUPS):
                 gather_words(o, g)
-        h1_grouped = keep.tile([P, PACK * (HALF + H1_SCALAR_COLS)], BF16, name="h1_grouped", align_bytes=64)
-        h1a_grouped = h1_grouped[:, : PACK * HALF]
-        h1b_grouped = h1_grouped[:, PACK * H1_SCALAR_COLS :]
-        round_h(h1a_grouped, h1a, HALF)
-        quantize_h(1, h1a_grouped, 0, HALF)
-        round_h(h1b_grouped, h1b, H1_SCALAR_COLS)
-        quantize_h(1, h1b_grouped, HALF, J)
-        for g, u, v in banks:
-            multiply(0, g, 2 * u, v)
-        for g, u, v in banks:
-            multiply(1, g, 2 * u, v)
-            for o in range(PASSES):
-                multiply(o, g, 2 * u + 1, v)
+        h0_grouped = keep.tile([P, PACK * J], BF16, name="h0_grouped", align_bytes=64)
+        interleave(nc.scalar.copy, h0_grouped[:], h0, J - H0_SCALAR_COLS, J)
+        interleave(nc.vector.tensor_copy, h0_grouped[:], h0, 0, HALF)
+        interleave(nc.vector.tensor_copy, h0_grouped[:], h0, HALF, J - H0_SCALAR_COLS)
+        quantize_h(0, 0, h0_grouped[:, : PACK * HALF])
+        quantize_h(0, 1, h0_grouped[:, PACK * HALF :])
+        h1_grouped = keep.tile([P, PACK * (HALF + H1_SCALAR_COLS[1])], BF16, name="h1_grouped", align_bytes=64)
+        for v in range(2):
+            first = PACK * H1_SCALAR_COLS[1] * v
+            grouped = h1_grouped[:, first : first + PACK * HALF]
+            interleave(nc.scalar.copy, grouped, h1[v], HALF - H1_SCALAR_COLS[v], HALF)
+            interleave(nc.vector.tensor_copy, grouped, h1[v], 0, HALF - H1_SCALAR_COLS[v])
+            quantize_h(1, v, grouped)
+        warm = psum.tile([P, SPAN], F32, name="warm")
+        for t in range(WARM_UPS):
+            nc.tensor.matmul_mx(
+                out=warm[:],
+                lhsT=x_codes[(0, 0)][:, t * P : (t + 1) * P].bitcast(FP8X4),
+                lhsT_scale=x_planes[0][:, t * P : (t + 1) * P],
+                rhs=x_codes[(1, 0)][:].bitcast(FP8X4),
+                rhs_scale=x_planes[0][:, :SPAN],
+                start=True,
+                stop=True,
+            )
+
+        def products(g):
+            for u in range(2):
+                for v in range(2):
+                    banks[(g, u, v)] = psum.tile([P, 2, HALF], F32, name="bank%d_%d" % (u, v))
+                    for o in range(PASSES):
+                        multiply(o, g, 2 * u, v)
+                        multiply(o, g, 2 * u + 1, v)
 
         y_planes = keep.tile([P, GROUPS, J], U8, name="y_planes", align_bytes=64)
         y_rows = [keep.tile([P, PACK, J], F32, name="y_rows%d" % g) for g in range(GROUPS)]
@@ -191,6 +197,7 @@ def tile_picked_znceg_sq_po_kernel(tc, x_words, x_scales, hT, label, offs, out_0
             )
 
         for g in range(GROUPS):
+            products(g)
             for v in range(2):
                 subtract(g, 0, v)
             store_rows(g, 0, 2)

@@ -114,7 +114,7 @@ def tile_picked_znceg_sq_po_kernel(tc, x_words, x_scales, hT, label, offs, out_0
 
         banks = {}
 
-        def multiply(o, g, t, v):
+        def multiply(o, g, t, v, start, stop):
             cols = slice(g * SPAN + t * P, g * SPAN + (t + 1) * P)
             nc.tensor.matmul_mx(
                 out=banks[(g, t // 2, v)][:, t % 2, :],
@@ -122,8 +122,8 @@ def tile_picked_znceg_sq_po_kernel(tc, x_words, x_scales, hT, label, offs, out_0
                 lhsT_scale=x_planes[o][:, cols],
                 rhs=h_codes[(o, v)][:].bitcast(FP8X4),
                 rhs_scale=h_planes[(o, v)][:],
-                start=(o == 0 and t % 2 == 0),
-                stop=(o == PASSES - 1 and t % 2 == 1),
+                start=start,
+                stop=stop,
             )
 
         for o in range(PASSES):
@@ -157,10 +157,12 @@ def tile_picked_znceg_sq_po_kernel(tc, x_words, x_scales, hT, label, offs, out_0
         def products(g):
             for u in range(2):
                 for v in range(2):
-                    banks[(g, u, v)] = psum.tile([P, 2, HALF], F32, name="bank%d_%d" % (u, v))
-                    for o in range(PASSES):
-                        multiply(o, g, 2 * u, v)
-                        multiply(o, g, 2 * u + 1, v)
+                    banks[(g, u, v)] = psum.tile([P, 2, HALF], F32, name="bank%d_%d" % ((2 * g + u) % 3, v))
+                    first, last = (0, 1) if g == 0 else (1, 0)
+                    multiply(first, g, 2 * u, v, True, False)
+                    multiply(first, g, 2 * u + 1, v, False, False)
+                    multiply(last, g, 2 * u, v, False, False)
+                    multiply(last, g, 2 * u + 1, v, False, True)
 
         y_planes = keep.tile([P, GROUPS, J], U8, name="y_planes", align_bytes=64)
         y_rows = [keep.tile([P, PACK, J], F32, name="y_rows%d" % g) for g in range(GROUPS)]

@@ -19,11 +19,10 @@ SPAN = P * PACK
 PASSES = K // SPAN
 GROUPS = S // SPAN
 QUADS = 4
-H0_SCALAR_COLS = 208
-H1_SCALAR_COLS = (128, 96)
-Y_SCALAR_COLS = 64
 HALF = J // 2
-WARM_UPS = 3
+H1_SCALAR_COLS = 88
+Y_SCALAR_COLS = 64
+EARLY_BANKS = 5
 
 
 def interleave(copy, grouped, rows, lo, hi):
@@ -40,40 +39,27 @@ def tile_picked_znceg_sq_po_kernel(tc, x_words, x_scales, hT, label, offs, out_0
         psum = ctx.enter_context(tc.psum_pool(name="psum", bufs=1))
 
         offsets = keep.tile([P, S // 16], U16, name="offsets")
-
         scale_table = keep.tile([P, T], U8, name="scale_table", align_bytes=64)
         nc.vector.memset(scale_table[:].bitcast(I32), 0)
         x_planes = [keep.tile([P, S], U8, name="x_plane%d" % o, align_bytes=64) for o in range(PASSES)]
         for plane in x_planes:
             nc.vector.memset(plane[:].bitcast(I32), 0)
 
-        word_table = [keep.tile([P, T], U32, name="word_table%d" % o, align_bytes=64) for o in range(PASSES)]
-
-        def load_words(o, lo, hi):
-            nc.sync.dma_start(
-                out=word_table[o][:, lo:hi].bitcast(I32),
-                in_=x_words[o].rearrange("p c t -> p (c t)")[:, PACK * lo : PACK * hi].bitcast(I32),
-            )
-
-        def load_rows(name, source, block, t_lo, t_hi, lo, hi):
-            rows = keep.tile([P, t_hi - t_lo, hi - lo], F32, name=name, align_bytes=64)
+        def load_rows(name, source, block, t_lo, t_hi):
+            rows = keep.tile([P, t_hi - t_lo, J], F32, name=name, align_bytes=64)
             dealt = source[block * SPAN : (block + 1) * SPAN, :].rearrange("(p t) j -> p t j", t=PACK)
-            nc.sync.dma_start(out=rows[:], in_=dealt[:, t_lo:t_hi, lo:hi])
+            nc.sync.dma_start(out=rows[:], in_=dealt[:, t_lo:t_hi, :])
             return rows
+
+        def load_words(o):
+            table = keep.tile([P, T], U32, name="word_table%d" % o, align_bytes=64)
+            nc.sync.dma_start(
+                out=table[:].bitcast(I32), in_=x_words[o].rearrange("p c t -> p (c t)").bitcast(I32)
+            )
+            return table
 
         picked_scales = keep.tile([P, S], U8, name="picked_scales", align_bytes=64)
         dealt_scales = keep.tile([P, S], U8, name="dealt_scales", align_bytes=64)
-
-        def load_scales():
-            nc.sync.dma_start(offsets[:], offs)
-            nc.sync.dma_start(
-                out=scale_table[0:P:4, :].bitcast(I32), in_=x_scales.rearrange("o q c -> (o q) c").bitcast(I32)
-            )
-            nc.vector.tensor_copy(picked_scales[:], scale_table[:].indirect(offsets[:]))
-            nc.vector.tensor_copy(
-                out=dealt_scales[:].rearrange("p (g t c i) -> p g c t i", g=GROUPS, t=PACK, i=16),
-                in_=picked_scales[:].rearrange("p (g c i t) -> p g c t i", g=GROUPS, t=PACK, i=16),
-            )
 
         def move_scales(o):
             for r in range(4):
@@ -82,87 +68,80 @@ def tile_picked_znceg_sq_po_kernel(tc, x_words, x_scales, hT, label, offs, out_0
                     in_=dealt_scales[64 * o + 4 * r : 64 * o + 64 : 16, :].bitcast(I32),
                 )
 
-        load_words(0, 0, T // 4)
-        load_scales()
-        load_words(0, T // 4, T)
-        load_words(1, 0, T)
+        h_rows = [load_rows("h0", hT, 0, 0, PACK)]
+        nc.sync.dma_start(offsets[:], offs)
+        nc.sync.dma_start(
+            out=scale_table[0:P:4, :].bitcast(I32), in_=x_scales.rearrange("o q c -> (o q) c").bitcast(I32)
+        )
+        nc.vector.tensor_copy(picked_scales[:], scale_table[:].indirect(offsets[:]))
+        nc.vector.tensor_copy(
+            out=dealt_scales[:].rearrange("p (g t c i) -> p g c t i", g=GROUPS, t=PACK, i=16),
+            in_=picked_scales[:].rearrange("p (g c i t) -> p g c t i", g=GROUPS, t=PACK, i=16),
+        )
+        word_table = [load_words(o) for o in range(PASSES)]
         move_scales(0)
-        h0 = load_rows("h0", hT, 0, 0, PACK, 0, J)
-        h1 = [load_rows("h1_%d" % v, hT, 1, 0, PACK, v * HALF, (v + 1) * HALF) for v in range(2)]
+        h_rows.append(load_rows("h1", hT, 1, 0, PACK))
         move_scales(1)
         label_pairs = [
-            [load_rows("label%d_%d" % (g, u), label, g, 2 * u, 2 * u + 2, 0, J) for u in range(2)]
+            [load_rows("label%d_%d" % (g, u), label, g, 2 * u, 2 * u + 2) for u in range(2)]
             for g in range(GROUPS)
         ]
 
         halves = [(o, v) for o in range(PASSES) for v in range(2)]
         h_codes = {ov: keep.tile([P, HALF], U32, name="h_codes%d_%d" % ov, align_bytes=64) for ov in halves}
         h_planes = {ov: keep.tile([P, HALF], U8, name="h_plane%d_%d" % ov, align_bytes=64) for ov in halves}
+        h_grouped = [
+            keep.tile([P, PACK * J], BF16, name="h_grouped%d" % o, align_bytes=64) for o in range(PASSES)
+        ]
 
-        def quantize_h(o, v, grouped):
-            nc.vector.quantize_mx(out=h_codes[(o, v)][:].bitcast(FP8X4), scales=h_planes[(o, v)][:], in_=grouped)
+        def quantize_h(o):
+            for v in range(2):
+                nc.vector.quantize_mx(
+                    out=h_codes[(o, v)][:].bitcast(FP8X4),
+                    scales=h_planes[(o, v)][:],
+                    in_=h_grouped[o][:, PACK * HALF * v : PACK * HALF * (v + 1)],
+                )
 
-        x_codes = {}
+        x_codes = [keep.tile([P, S], U32, name="x_codes%d" % o, align_bytes=64) for o in range(PASSES)]
 
-        def gather_words(o, g):
-            codes = keep.tile([P, SPAN], U32, name="x_codes%d_%d" % (o, g), align_bytes=64)
+        def gather_words(o):
             nc.vector.tensor_copy(
-                codes[:].rearrange("p (t m) -> p m t", t=PACK),
-                word_table[o][:].indirect(offsets[:, g * (SPAN // 16) : (g + 1) * (SPAN // 16)]),
-            )
-            x_codes[(o, g)] = codes
-
-        banks = {}
-
-        def multiply(o, g, t, v, start, stop):
-            cols = slice(g * SPAN + t * P, g * SPAN + (t + 1) * P)
-            nc.tensor.matmul_mx(
-                out=banks[(g, t // 2, v)][:, t % 2, :],
-                lhsT=x_codes[(o, g)][:, t * P : (t + 1) * P].bitcast(FP8X4),
-                lhsT_scale=x_planes[o][:, cols],
-                rhs=h_codes[(o, v)][:].bitcast(FP8X4),
-                rhs_scale=h_planes[(o, v)][:],
-                start=start,
-                stop=stop,
+                x_codes[o][:].rearrange("p (g t m) -> p g m t", g=GROUPS, t=PACK),
+                word_table[o][:].indirect(offsets[:]),
             )
 
-        for o in range(PASSES):
-            for g in range(GROUPS):
-                gather_words(o, g)
-        h0_grouped = keep.tile([P, PACK * J], BF16, name="h0_grouped", align_bytes=64)
-        interleave(nc.scalar.copy, h0_grouped[:], h0, J - H0_SCALAR_COLS, J)
-        interleave(nc.vector.tensor_copy, h0_grouped[:], h0, 0, HALF)
-        interleave(nc.vector.tensor_copy, h0_grouped[:], h0, HALF, J - H0_SCALAR_COLS)
-        quantize_h(0, 0, h0_grouped[:, : PACK * HALF])
-        quantize_h(0, 1, h0_grouped[:, PACK * HALF :])
-        h1_grouped = keep.tile([P, PACK * (HALF + H1_SCALAR_COLS[1])], BF16, name="h1_grouped", align_bytes=64)
-        for v in range(2):
-            first = PACK * H1_SCALAR_COLS[1] * v
-            grouped = h1_grouped[:, first : first + PACK * HALF]
-            interleave(nc.scalar.copy, grouped, h1[v], HALF - H1_SCALAR_COLS[v], HALF)
-            interleave(nc.vector.tensor_copy, grouped, h1[v], 0, HALF - H1_SCALAR_COLS[v])
-            quantize_h(1, v, grouped)
-        warm = psum.tile([P, SPAN], F32, name="warm")
-        for t in range(WARM_UPS):
-            nc.tensor.matmul_mx(
-                out=warm[:],
-                lhsT=x_codes[(0, 0)][:, t * P : (t + 1) * P].bitcast(FP8X4),
-                lhsT_scale=x_planes[0][:, t * P : (t + 1) * P],
-                rhs=x_codes[(1, 0)][:].bitcast(FP8X4),
-                rhs_scale=x_planes[0][:, :SPAN],
-                start=True,
-                stop=True,
-            )
+        pairs = [(g, u, v) for g in range(GROUPS) for u in range(2) for v in range(2)]
+        banks = {guv: psum.tile([P, 2, HALF], F32, name="bank%d_%d_%d" % guv) for guv in pairs}
 
-        def products(g):
-            for u in range(2):
-                for v in range(2):
-                    banks[(g, u, v)] = psum.tile([P, 2, HALF], F32, name="bank%d_%d" % ((2 * g + u) % 3, v))
-                    first, last = (0, 1) if g == 0 else (1, 0)
-                    multiply(first, g, 2 * u, v, True, False)
-                    multiply(first, g, 2 * u + 1, v, False, False)
-                    multiply(last, g, 2 * u, v, False, False)
-                    multiply(last, g, 2 * u + 1, v, False, True)
+        def multiply(o, which, opens):
+            for g, u, v in which:
+                for e in range(2):
+                    first = g * SPAN + (2 * u + e) * P
+                    nc.tensor.matmul_mx(
+                        out=banks[(g, u, v)][:, e, :],
+                        lhsT=x_codes[o][:, first : first + P].bitcast(FP8X4),
+                        lhsT_scale=x_planes[o][:, first : first + P],
+                        rhs=h_codes[(o, v)][:].bitcast(FP8X4),
+                        rhs_scale=h_planes[(o, v)][:],
+                        start=(opens and e == 0),
+                        stop=(not opens and e == 1),
+                    )
+
+        interleave(nc.scalar.copy, h_grouped[0][:], h_rows[0], 0, J)
+        quantize_h(0)
+        gather_words(0)
+        gather_words(1)
+        early, late = pairs[:EARLY_BANKS], pairs[EARLY_BANKS:]
+        multiply(0, early, True)
+        for lo in (0, HALF):
+            split = lo + HALF - H1_SCALAR_COLS
+            interleave(nc.scalar.copy, h_grouped[1][:], h_rows[1], split, lo + HALF)
+            interleave(nc.vector.tensor_copy, h_grouped[1][:], h_rows[1], lo, split)
+        quantize_h(1)
+        multiply(1, early, False)
+        for guv in late:
+            multiply(1, [guv], True)
+            multiply(0, [guv], False)
 
         y_planes = keep.tile([P, GROUPS, J], U8, name="y_planes", align_bytes=64)
         y_rows = [keep.tile([P, PACK, J], F32, name="y_rows%d" % g) for g in range(GROUPS)]
@@ -199,7 +178,6 @@ def tile_picked_znceg_sq_po_kernel(tc, x_words, x_scales, hT, label, offs, out_0
             )
 
         for g in range(GROUPS):
-            products(g)
             for v in range(2):
                 subtract(g, 0, v)
             store_rows(g, 0, 2)

@@ -20,9 +20,9 @@ PASSES = K // SPAN
 GROUPS = S // SPAN
 QUADS = 4
 HALF = J // 2
-H1_SCALAR_COLS = 88
+H1_SCALAR_COLS = 144
 Y_SCALAR_COLS = 64
-EARLY_BANKS = 5
+EARLY_BANKS = 4
 
 
 def interleave(copy, grouped, rows, lo, hi):
@@ -45,10 +45,10 @@ def tile_picked_znceg_sq_po_kernel(tc, x_words, x_scales, hT, label, offs, out_0
         for plane in x_planes:
             nc.vector.memset(plane[:].bitcast(I32), 0)
 
-        def load_rows(name, source, block, t_lo, t_hi):
-            rows = keep.tile([P, t_hi - t_lo, J], F32, name=name, align_bytes=64)
+        def load_rows(name, source, block, t_lo, t_hi, lo=0, hi=J):
+            rows = keep.tile([P, t_hi - t_lo, hi - lo], F32, name=name, align_bytes=64)
             dealt = source[block * SPAN : (block + 1) * SPAN, :].rearrange("(p t) j -> p t j", t=PACK)
-            nc.sync.dma_start(out=rows[:], in_=dealt[:, t_lo:t_hi, :])
+            nc.sync.dma_start(out=rows[:], in_=dealt[:, t_lo:t_hi, lo:hi])
             return rows
 
         def load_words(o):
@@ -64,14 +64,14 @@ def tile_picked_znceg_sq_po_kernel(tc, x_words, x_scales, hT, label, offs, out_0
         def move_scales(o):
             for r in range(4):
                 nc.sync.dma_start(
-                    out=x_planes[o][r:P:32, :].bitcast(I32),
-                    in_=dealt_scales[64 * o + 4 * r : 64 * o + 64 : 16, :].bitcast(I32),
+                    out=x_planes[o][4 * o + r : P : 32, :].bitcast(I32),
+                    in_=dealt_scales[32 + 32 * o + 2 * r : 64 + 32 * o : 8, :].bitcast(I32),
                 )
 
-        h_rows = [load_rows("h0", hT, 0, 0, PACK)]
+        h0 = load_rows("h0", hT, 0, 0, PACK)
         nc.sync.dma_start(offsets[:], offs)
         nc.sync.dma_start(
-            out=scale_table[0:P:4, :].bitcast(I32), in_=x_scales.rearrange("o q c -> (o q) c").bitcast(I32)
+            out=scale_table[32:96:2, :].bitcast(I32), in_=x_scales.rearrange("o q c -> (o q) c").bitcast(I32)
         )
         nc.vector.tensor_copy(picked_scales[:], scale_table[:].indirect(offsets[:]))
         nc.vector.tensor_copy(
@@ -80,7 +80,7 @@ def tile_picked_znceg_sq_po_kernel(tc, x_words, x_scales, hT, label, offs, out_0
         )
         word_table = [load_words(o) for o in range(PASSES)]
         move_scales(0)
-        h_rows.append(load_rows("h1", hT, 1, 0, PACK))
+        h1 = [load_rows("h1_%d" % v, hT, 1, 0, PACK, v * HALF, (v + 1) * HALF) for v in range(2)]
         move_scales(1)
         label_pairs = [
             [load_rows("label%d_%d" % (g, u), label, g, 2 * u, 2 * u + 2) for u in range(2)]
@@ -90,17 +90,9 @@ def tile_picked_znceg_sq_po_kernel(tc, x_words, x_scales, hT, label, offs, out_0
         halves = [(o, v) for o in range(PASSES) for v in range(2)]
         h_codes = {ov: keep.tile([P, HALF], U32, name="h_codes%d_%d" % ov, align_bytes=64) for ov in halves}
         h_planes = {ov: keep.tile([P, HALF], U8, name="h_plane%d_%d" % ov, align_bytes=64) for ov in halves}
-        h_grouped = [
-            keep.tile([P, PACK * J], BF16, name="h_grouped%d" % o, align_bytes=64) for o in range(PASSES)
-        ]
 
-        def quantize_h(o):
-            for v in range(2):
-                nc.vector.quantize_mx(
-                    out=h_codes[(o, v)][:].bitcast(FP8X4),
-                    scales=h_planes[(o, v)][:],
-                    in_=h_grouped[o][:, PACK * HALF * v : PACK * HALF * (v + 1)],
-                )
+        def quantize_h(o, v, grouped):
+            nc.vector.quantize_mx(out=h_codes[(o, v)][:].bitcast(FP8X4), scales=h_planes[(o, v)][:], in_=grouped)
 
         x_codes = [keep.tile([P, S], U32, name="x_codes%d" % o, align_bytes=64) for o in range(PASSES)]
 
@@ -120,24 +112,29 @@ def tile_picked_znceg_sq_po_kernel(tc, x_words, x_scales, hT, label, offs, out_0
                     nc.tensor.matmul_mx(
                         out=banks[(g, u, v)][:, e, :],
                         lhsT=x_codes[o][:, first : first + P].bitcast(FP8X4),
-                        lhsT_scale=x_planes[o][:, first : first + P],
+                        lhsT_scale=x_planes[o][4 * o :, first : first + P],
                         rhs=h_codes[(o, v)][:].bitcast(FP8X4),
                         rhs_scale=h_planes[(o, v)][:],
                         start=(opens and e == 0),
                         stop=(not opens and e == 1),
                     )
 
-        interleave(nc.scalar.copy, h_grouped[0][:], h_rows[0], 0, J)
-        quantize_h(0)
+        h0_grouped = keep.tile([P, PACK * J], BF16, name="h0_grouped", align_bytes=64)
+        interleave(nc.scalar.copy, h0_grouped[:], h0, 0, J)
+        for v in range(2):
+            quantize_h(0, v, h0_grouped[:, PACK * HALF * v : PACK * HALF * (v + 1)])
         gather_words(0)
         gather_words(1)
         early, late = pairs[:EARLY_BANKS], pairs[EARLY_BANKS:]
         multiply(0, early, True)
-        for lo in (0, HALF):
-            split = lo + HALF - H1_SCALAR_COLS
-            interleave(nc.scalar.copy, h_grouped[1][:], h_rows[1], split, lo + HALF)
-            interleave(nc.vector.tensor_copy, h_grouped[1][:], h_rows[1], lo, split)
-        quantize_h(1)
+        h1_grouped = [
+            keep.tile([P, PACK * HALF], BF16, name="h1_grouped%d" % v, align_bytes=64) for v in range(2)
+        ]
+        interleave(nc.scalar.copy, h1_grouped[0][:], h1[0], 0, HALF)
+        interleave(nc.scalar.copy, h1_grouped[1][:], h1[1], HALF - H1_SCALAR_COLS, HALF)
+        interleave(nc.vector.tensor_copy, h1_grouped[1][:], h1[1], 0, HALF - H1_SCALAR_COLS)
+        for v in range(2):
+            quantize_h(1, v, h1_grouped[v][:])
         multiply(1, early, False)
         for guv in late:
             multiply(1, [guv], True)
@@ -195,8 +192,7 @@ def tile_picked_znceg_sq_po_kernel(tc, x_words, x_scales, hT, label, offs, out_0
         quantize_y(1, HALF, J)
         store_codes(1)
         for r in range(4):
-            queue = nc.sync if r == 0 else nc.scalar
-            queue.dma_start(
+            nc.scalar.dma_start(
                 out=out_2[:, r : 4 * QUADS : 4, :].rearrange("g q c -> q g c").bitcast(I32),
                 in_=y_planes[r:P:32, :, :].bitcast(I32),
             )

@@ -20,9 +20,8 @@ PASSES = K // SPAN
 GROUPS = S // SPAN
 QUADS = 4
 HALF = J // 2
-H1_SCALAR_COLS = 144
+H1_SCALAR_COLS = 128
 Y_SCALAR_COLS = 64
-EARLY_BANKS = 4
 
 
 def interleave(copy, grouped, rows, lo, hi):
@@ -68,7 +67,7 @@ def tile_picked_znceg_sq_po_kernel(tc, x_words, x_scales, hT, label, offs, out_0
                     in_=dealt_scales[32 + 32 * o + 2 * r : 64 + 32 * o : 8, :].bitcast(I32),
                 )
 
-        h0 = load_rows("h0", hT, 0, 0, PACK)
+        h1 = [load_rows("h1_0", hT, 1, 0, PACK, 0, HALF)]
         nc.sync.dma_start(offsets[:], offs)
         nc.sync.dma_start(
             out=scale_table[32:96:2, :].bitcast(I32), in_=x_scales.rearrange("o q c -> (o q) c").bitcast(I32)
@@ -79,9 +78,10 @@ def tile_picked_znceg_sq_po_kernel(tc, x_words, x_scales, hT, label, offs, out_0
             in_=picked_scales[:].rearrange("p (g c i t) -> p g c t i", g=GROUPS, t=PACK, i=16),
         )
         word_table = [load_words(o) for o in range(PASSES)]
-        move_scales(0)
-        h1 = [load_rows("h1_%d" % v, hT, 1, 0, PACK, v * HALF, (v + 1) * HALF) for v in range(2)]
         move_scales(1)
+        h0 = load_rows("h0", hT, 0, 0, PACK)
+        h1.append(load_rows("h1_1", hT, 1, 0, PACK, HALF, J))
+        move_scales(0)
         label_pairs = [
             [load_rows("label%d_%d" % (g, u), label, g, 2 * u, 2 * u + 2) for u in range(2)]
             for g in range(GROUPS)
@@ -94,13 +94,17 @@ def tile_picked_znceg_sq_po_kernel(tc, x_words, x_scales, hT, label, offs, out_0
         def quantize_h(o, v, grouped):
             nc.vector.quantize_mx(out=h_codes[(o, v)][:].bitcast(FP8X4), scales=h_planes[(o, v)][:], in_=grouped)
 
-        x_codes = [keep.tile([P, S], U32, name="x_codes%d" % o, align_bytes=64) for o in range(PASSES)]
+        x_codes = [
+            [keep.tile([P, SPAN], U32, name="x_codes%d_%d" % (o, g), align_bytes=64) for g in range(GROUPS)]
+            for o in range(PASSES)
+        ]
 
         def gather_words(o):
-            nc.vector.tensor_copy(
-                x_codes[o][:].rearrange("p (g t m) -> p g m t", g=GROUPS, t=PACK),
-                word_table[o][:].indirect(offsets[:]),
-            )
+            for g in range(GROUPS):
+                nc.vector.tensor_copy(
+                    x_codes[o][g][:].rearrange("p (t m) -> p m t", t=PACK),
+                    word_table[o][:].indirect(offsets[:, g * (SPAN // 16) : (g + 1) * (SPAN // 16)]),
+                )
 
         pairs = [(g, u, v) for g in range(GROUPS) for u in range(2) for v in range(2)]
         banks = {guv: psum.tile([P, 2, HALF], F32, name="bank%d_%d_%d" % guv) for guv in pairs}
@@ -108,10 +112,11 @@ def tile_picked_znceg_sq_po_kernel(tc, x_words, x_scales, hT, label, offs, out_0
         def multiply(o, which, opens):
             for g, u, v in which:
                 for e in range(2):
-                    first = g * SPAN + (2 * u + e) * P
+                    t = 2 * u + e
+                    first = g * SPAN + t * P
                     nc.tensor.matmul_mx(
                         out=banks[(g, u, v)][:, e, :],
-                        lhsT=x_codes[o][:, first : first + P].bitcast(FP8X4),
+                        lhsT=x_codes[o][g][:, t * P : (t + 1) * P].bitcast(FP8X4),
                         lhsT_scale=x_planes[o][4 * o :, first : first + P],
                         rhs=h_codes[(o, v)][:].bitcast(FP8X4),
                         rhs_scale=h_planes[(o, v)][:],
@@ -120,25 +125,28 @@ def tile_picked_znceg_sq_po_kernel(tc, x_words, x_scales, hT, label, offs, out_0
                     )
 
         h0_grouped = keep.tile([P, PACK * J], BF16, name="h0_grouped", align_bytes=64)
-        interleave(nc.scalar.copy, h0_grouped[:], h0, 0, J)
-        for v in range(2):
-            quantize_h(0, v, h0_grouped[:, PACK * HALF * v : PACK * HALF * (v + 1)])
-        gather_words(0)
-        gather_words(1)
-        early, late = pairs[:EARLY_BANKS], pairs[EARLY_BANKS:]
-        multiply(0, early, True)
         h1_grouped = [
             keep.tile([P, PACK * HALF], BF16, name="h1_grouped%d" % v, align_bytes=64) for v in range(2)
         ]
         interleave(nc.scalar.copy, h1_grouped[0][:], h1[0], 0, HALF)
+        quantize_h(1, 0, h1_grouped[0][:])
+        gather_words(0)
+        gather_words(1)
+        first_halves = [guv for guv in pairs if guv[2] == 0]
+        multiply(1, first_halves, True)
+        interleave(nc.scalar.copy, h0_grouped[:], h0, HALF, J)
+        interleave(nc.vector.tensor_copy, h0_grouped[:], h0, 0, HALF)
+        quantize_h(0, 0, h0_grouped[:, : PACK * HALF])
         interleave(nc.scalar.copy, h1_grouped[1][:], h1[1], HALF - H1_SCALAR_COLS, HALF)
         interleave(nc.vector.tensor_copy, h1_grouped[1][:], h1[1], 0, HALF - H1_SCALAR_COLS)
-        for v in range(2):
-            quantize_h(1, v, h1_grouped[v][:])
-        multiply(1, early, False)
-        for guv in late:
-            multiply(1, [guv], True)
-            multiply(0, [guv], False)
+        quantize_h(0, 1, h0_grouped[:, PACK * HALF :])
+        quantize_h(1, 1, h1_grouped[1][:])
+        for guv in pairs:
+            if guv in first_halves:
+                multiply(0, [guv], False)
+            else:
+                multiply(0, [guv], True)
+                multiply(1, [guv], False)
 
         y_planes = keep.tile([P, GROUPS, J], U8, name="y_planes", align_bytes=64)
         y_rows = [keep.tile([P, PACK, J], F32, name="y_rows%d" % g) for g in range(GROUPS)]

from contextlib import ExitStack

import concourse.mybir as mybir

K, T, S, J = 1024, 4096, 1024, 512
FLOPS = 2 * K * S * J

F32 = mybir.dt.float32
BF16 = mybir.dt.bfloat16
I32 = mybir.dt.int32
U32 = mybir.dt.uint32
U16 = mybir.dt.uint16
U8 = mybir.dt.uint8
FP8X4 = mybir.dt.float8_e4m3fn_x4

P = 128
PACK = 4
SPAN = P * PACK
PASSES = K // SPAN
GROUPS = S // SPAN
QUADS = 4
HALF = J // 2
H1_SCALAR_COLS = 128
Y_SCALAR_COLS = 64


def interleave(copy, grouped, rows, lo, hi):
    copy(
        out=grouped[:, PACK * lo : PACK * hi].rearrange("p (c i t) -> p c t i", i=4, t=PACK),
        in_=rows[:, :, lo:hi].rearrange("p t (c i) -> p c t i", i=4),
    )


def tile_picked_znceg_sq_po_kernel(tc, x_words, x_scales, hT, label, offs, out_0, out_1, out_2):
    nc = tc.nc
    with ExitStack() as ctx:
        keep = ctx.enter_context(tc.tile_pool(name="keep", bufs=1))
        psum = ctx.enter_context(tc.psum_pool(name="psum", bufs=1))

        offsets = keep.tile([P, S // 16], U16, name="offsets")
        scale_table = keep.tile([P, T], U8, name="scale_table", align_bytes=64)
        nc.vector.memset(scale_table[:].bitcast(I32), 0)
        x_planes = [keep.tile([P, S], U8, name="x_plane%d" % o, align_bytes=64) for o in range(PASSES)]
        for plane in x_planes:
            nc.vector.memset(plane[:].bitcast(I32), 0)

        def load_rows(name, source, block, t_lo, t_hi, lo=0, hi=J):
            rows = keep.tile([P, t_hi - t_lo, hi - lo], F32, name=name, align_bytes=64)
            dealt = source[block * SPAN : (block + 1) * SPAN, :].rearrange("(p t) j -> p t j", t=PACK)
            nc.sync.dma_start(out=rows[:], in_=dealt[:, t_lo:t_hi, lo:hi])
            return rows

        def load_words(o):
            table = keep.tile([P, T], U32, name="word_table%d" % o, align_bytes=64)
            nc.sync.dma_start(
                out=table[:].bitcast(I32), in_=x_words[o].rearrange("p c t -> p (c t)").bitcast(I32)
            )
            return table

        picked_scales = keep.tile([P, S], U8, name="picked_scales", align_bytes=64)
        dealt_scales = keep.tile([P, S], U8, name="dealt_scales", align_bytes=64)

        def move_scales(o):
            for r in range(4):
                nc.sync.dma_start(
                    out=x_planes[o][4 * o + r : P : 32, :].bitcast(I32),
                    in_=dealt_scales[32 + 32 * o + 2 * r : 64 + 32 * o : 8, :].bitcast(I32),
                )

        h1 = [load_rows("h1_0", hT, 1, 0, PACK, 0, HALF)]
        nc.sync.dma_start(offsets[:], offs)
        nc.sync.dma_start(
            out=scale_table[32:96:2, :].bitcast(I32), in_=x_scales.rearrange("o q c -> (o q) c").bitcast(I32)
        )
        nc.vector.tensor_copy(picked_scales[:], scale_table[:].indirect(offsets[:]))
        nc.vector.tensor_copy(
            out=dealt_scales[:].rearrange("p (g t c i) -> p g c t i", g=GROUPS, t=PACK, i=16),
            in_=picked_scales[:].rearrange("p (g c i t) -> p g c t i", g=GROUPS, t=PACK, i=16),
        )
        word_table = [load_words(o) for o in range(PASSES)]
        move_scales(1)
        h0 = load_rows("h0", hT, 0, 0, PACK)
        h1.append(load_rows("h1_1", hT, 1, 0, PACK, HALF, J))
        move_scales(0)
        label_pairs = [
            [load_rows("label%d_%d" % (g, u), label, g, 2 * u, 2 * u + 2) for u in range(2)]
            for g in range(GROUPS)
        ]

        halves = [(o, v) for o in range(PASSES) for v in range(2)]
        h_codes = {ov: keep.tile([P, HALF], U32, name="h_codes%d_%d" % ov, align_bytes=64) for ov in halves}
        h_planes = {ov: keep.tile([P, HALF], U8, name="h_plane%d_%d" % ov, align_bytes=64) for ov in halves}

        def quantize_h(o, v, grouped):
            nc.vector.quantize_mx(out=h_codes[(o, v)][:].bitcast(FP8X4), scales=h_planes[(o, v)][:], in_=grouped)

        x_codes = [
            [keep.tile([P, SPAN], U32, name="x_codes%d_%d" % (o, g), align_bytes=64) for g in range(GROUPS)]
            for o in range(PASSES)
        ]

        def gather_words(o):
            for g in range(GROUPS):
                nc.vector.tensor_copy(
                    x_codes[o][g][:].rearrange("p (t m) -> p m t", t=PACK),
                    word_table[o][:].indirect(offsets[:, g * (SPAN // 16) : (g + 1) * (SPAN // 16)]),
                )

        pairs = [(g, u, v) for g in range(GROUPS) for u in range(2) for v in range(2)]
        banks = {guv: psum.tile([P, 2, HALF], F32, name="bank%d_%d_%d" % guv) for guv in pairs}

        def multiply(o, which, opens):
            for g, u, v in which:
                for e in range(2):
                    t = 2 * u + e
                    first = g * SPAN + t * P
                    nc.tensor.matmul_mx(
                        out=banks[(g, u, v)][:, e, :],
                        lhsT=x_codes[o][g][:, t * P : (t + 1) * P].bitcast(FP8X4),
                        lhsT_scale=x_planes[o][4 * o :, first : first + P],
                        rhs=h_codes[(o, v)][:].bitcast(FP8X4),
                        rhs_scale=h_planes[(o, v)][:],
                        start=(opens and e == 0),
                        stop=(not opens and e == 1),
                    )

        h0_grouped = keep.tile([P, PACK * J], BF16, name="h0_grouped", align_bytes=64)
        h1_grouped = [
            keep.tile([P, PACK * HALF], BF16, name="h1_grouped%d" % v, align_bytes=64) for v in range(2)
        ]
        interleave(nc.scalar.copy, h1_grouped[0][:], h1[0], 0, HALF)
        quantize_h(1, 0, h1_grouped[0][:])
        gather_words(0)
        gather_words(1)
        first_halves = [guv for guv in pairs if guv[2] == 0]
        multiply(1, first_halves, True)
        interleave(nc.scalar.copy, h0_grouped[:], h0, HALF, J)
        interleave(nc.vector.tensor_copy, h0_grouped[:], h0, 0, HALF)
        quantize_h(0, 0, h0_grouped[:, : PACK * HALF])
        interleave(nc.scalar.copy, h1_grouped[1][:], h1[1], HALF - H1_SCALAR_COLS, HALF)
        interleave(nc.vector.tensor_copy, h1_grouped[1][:], h1[1], 0, HALF - H1_SCALAR_COLS)
        quantize_h(0, 1, h0_grouped[:, PACK * HALF :])
        quantize_h(1, 1, h1_grouped[1][:])
        for guv in pairs:
            if guv in first_halves:
                multiply(0, [guv], False)
            else:
                multiply(0, [guv], True)
                multiply(1, [guv], False)

        y_planes = keep.tile([P, GROUPS, J], U8, name="y_planes", align_bytes=64)
        y_rows = [keep.tile([P, PACK, J], F32, name="y_rows%d" % g) for g in range(GROUPS)]
        y_grouped = [
            keep.tile([P, PACK * J], BF16, name="y_grouped%d" % g, align_bytes=64) for g in range(GROUPS)
        ]
        y_codes = [keep.tile([P, J], U32, name="y_codes%d" % g, align_bytes=64) for g in range(GROUPS)]

        def subtract(g, u, v):
            half = slice(v * HALF, (v + 1) * HALF)
            nc.vector.tensor_sub(
                out=y_rows[g][:, 2 * u : 2 * u + 2, half],
                in0=banks[(g, u, v)][:],
                in1=label_pairs[g][u][:, :, half],
            )

        def store_rows(g, lo, hi):
            stored = out_0[g * SPAN : (g + 1) * SPAN, :].rearrange("(p t) j -> p t j", t=PACK)
            nc.sync.dma_start(out=stored[:, lo:hi, :], in_=y_rows[g][:, lo:hi, :])

        def round_y(copy, g, lo, hi):
            interleave(copy, y_grouped[g][:], y_rows[g], lo, hi)

        def quantize_y(g, lo, hi):
            nc.vector.quantize_mx(
                out=y_codes[g][:, lo:hi].bitcast(FP8X4),
                scales=y_planes[:, g, lo:hi],
                in_=y_grouped[g][:, PACK * lo : PACK * hi],
            )

        def store_codes(g):
            nc.sync.dma_start(
                out=out_1[g].rearrange("p c t -> p (c t)").bitcast(I32), in_=y_codes[g][:].bitcast(I32)
            )

        for g in range(GROUPS):
            for v in range(2):
                subtract(g, 0, v)
            store_rows(g, 0, 2)
            subtract(g, 1, 0)
            round_y(nc.scalar.copy, g, 0, HALF)
            subtract(g, 1, 1)
            store_rows(g, 2, PACK)
            if g == 0:
                round_y(nc.scalar.copy, g, HALF, J)
        quantize_y(0, 0, J)
        store_codes(0)
        round_y(nc.scalar.copy, 1, J - Y_SCALAR_COLS, J)
        round_y(nc.vector.tensor_copy, 1, HALF, J - Y_SCALAR_COLS)
        quantize_y(1, 0, HALF)
        quantize_y(1, HALF, J)
        store_codes(1)
        for r in range(4):
            nc.scalar.dma_start(
                out=out_2[:, r : 4 * QUADS : 4, :].rearrange("g q c -> q g c").bitcast(I32),
                in_=y_planes[r:P:32, :, :].bitcast(I32),
            )
